import numpy as np
import ml_dtypes


def mxq(x, axis, fmt="e4m3"):
    dtype, down = {"e4m3": (ml_dtypes.float8_e4m3fn, 7), "e5m2": (ml_dtypes.float8_e5m2, 14)}[fmt]
    v = np.moveaxis(np.asarray(x, np.float32).astype(ml_dtypes.bfloat16).astype(np.float64), axis, -1)
    blocks = v.reshape(v.shape[:-1] + (-1, 32))
    amax = np.abs(blocks).max(-1, keepdims=True)
    byte = np.maximum(np.where(amax > 0, np.frexp(amax)[1] - 1 + 127, 0) - down, 1)
    scale = np.exp2(byte - 127.0)
    codes = (blocks / scale).astype(np.float32).astype(dtype).astype(np.float64)
    return np.moveaxis((codes * scale).reshape(v.shape), -1, axis)


WIDE = False


def mx_kscale(k):
    if not WIDE:
        return np.ones(k)
    levels = np.array([10, -10, 5, -5, 0])
    if k % 512:
        return np.exp2(np.random.permutation(np.resize(levels, k // 32))).repeat(32)
    a = np.empty((k // 512, 16))
    for p in range(k // 512):
        a[p, :8] = np.random.permutation(np.resize(levels, 8))
        for g in range(8):
            far = levels[np.abs(levels - a[p, g]) >= 10]
            a[p, g + 8] = far[np.random.randint(len(far))]
    return np.exp2(a.ravel()).repeat(32)


def f64(x):
    return np.asarray(x).astype(np.float64)


def striped(idx):
    return np.tile(idx.reshape(-1, 16).T, (8, 1)).astype(np.uint16)


def unstriped(offs):
    return offs[:16].T.reshape(-1).astype(np.int64)


def striped8(idx):
    return np.concatenate([x.reshape(-1, 16).T for x in idx]).astype(np.uint16)


def runs(offs, k):
    lists = np.stack([offs[16 * r : 16 * r + 16].T.reshape(-1) for r in range(8)]).astype(np.int64)
    return lists[np.arange(k) % 512 // 64]


def pack_weight(w):
    k, n = w.shape
    w = f64(np.asarray(w, np.float32).astype(ml_dtypes.bfloat16)).reshape(k // 32, 32, n)
    amax = np.abs(w).max(1)
    byte = np.clip(np.where(amax > 0, np.frexp(amax)[1] - 1 + 127 - 7, 1), 1, 254)
    scaled = (w * np.exp2(127.0 - byte)[:, None, :]).reshape(k, n).astype(np.float32)
    words = np.ascontiguousarray(scaled.reshape(k // 512, 128, 4, n).transpose(0, 1, 3, 2)).astype(ml_dtypes.float8_e4m3fn).view(np.uint8)
    return words, np.ascontiguousarray(byte.astype(np.uint8).reshape(k // 512, 16, n))


def unpack_weight(words, scales):
    g, p, n, _ = words.shape
    vals = np.ascontiguousarray(words).view(ml_dtypes.float8_e4m3fn).astype(np.float64) * np.repeat(np.exp2(scales.astype(np.float64) - 127.0), 8, axis=1)[..., None]
    return vals.transpose(0, 1, 3, 2).reshape(g * 512, n)

def planes(y):
    n, m = y.shape
    v = y.astype(np.float32).astype(ml_dtypes.bfloat16).astype(np.float64).reshape(n // 32, 32, m)
    top = np.abs(v).max(1)
    byte = np.clip(np.where(top > 0, np.frexp(top)[1] - 1 + 127 - 7, 1), 1, 254)
    codes = (v * np.exp2(127.0 - byte)[:, None, :]).reshape(n, m).astype(np.float32).astype(ml_dtypes.float8_e4m3fn).view(np.uint8)
    words = codes.reshape(n // 512, 128, 4, m).transpose(0, 1, 3, 2)
    return np.ascontiguousarray(words), np.ascontiguousarray(byte.astype(np.uint8).reshape(n // 512, 16, m))


K, T, S, N, G, H = 512, 2048, 512, 512, 2048, 512


def setup_inputs():
    n = np.random.standard_normal
    s = mx_kscale(K)[:, None]
    u = mx_kscale(S)
    packed_xT = pack_weight(n((K, T)) * s)
    packed_dT = pack_weight(n((K, G)) / s)
    packed_w1 = pack_weight(n((H, N)) / np.sqrt(H) / u[:, None])
    return {
        "x_words": packed_xT[0],
        "x_scales": packed_xT[1],
        "d_words": packed_dT[0],
        "d_scales": packed_dT[1],
        "gn": (np.random.uniform(0.5, 1.5, (H, 1)) * u[:, None]).astype(np.float32),
        "w1_words": packed_w1[0],
        "w1_scales": packed_w1[1],
        "offs": striped(np.random.permutation(T)[:S]),
        "kidx": striped8(np.random.randint(0, G, (8, H))),
        "n1": striped8(np.stack([np.random.permutation(S) for _ in range(8)])),
        "n2": striped8(np.stack([np.random.permutation(S) for _ in range(8)])),
    }


def reference(x_words, x_scales, d_words, d_scales, gn, w1_words, w1_scales, offs, kidx, n1, n2):
    d_kidx = unpack_weight(d_words, d_scales)[np.arange(K)[:, None], runs(kidx, K)]
    xq = unpack_weight(x_words, x_scales)[:, unstriped(offs)]
    s = 0.0625 * (d_kidx.T @ xq)
    z = f64(gn) * (s - (s[np.arange(H)[:, None], runs(n1, H)]))
    h = unpack_weight(w1_words, w1_scales).T @ mxq(z, 0, "e4m3")
    out_0 = np.maximum(h, h[np.arange(N)[:, None], runs(n2, N)])
    return (out_0,) + planes(out_0)

@@ -1,0 +1,201 @@
+from contextlib import ExitStack
+
+import concourse.mybir as mybir
+
+K, T, S, N, G, H = 512, 2048, 512, 512, 2048, 512
+FLOPS = 2 * K * H * S + 2 * H * N * S
+
+F32 = mybir.dt.float32
+BF16 = mybir.dt.bfloat16
+I32 = mybir.dt.int32
+U32 = mybir.dt.uint32
+U16 = mybir.dt.uint16
+U8 = mybir.dt.uint8
+FP8X4 = mybir.dt.float8_e4m3fn_x4
+COPY = mybir.ActivationFunctionType.Copy
+ALU = mybir.AluOpType
+
+P = 128
+PACK = 4
+HALF = S // 2
+PIECES1 = ((0, 256), (256, 384), (384, 512))
+PIECES2 = ((0, 256), (256, 384), (384, 512))
+
+
+def words_view(ap):
+    return ap[0].rearrange("p n r -> p (n r)").bitcast(I32)
+
+
+def rows_of_blocks(ap):
+    rows = ap[0].bitcast(I32)
+    return rows.unsqueeze(1).to_broadcast([16, 8, rows.shape[1]])
+
+
+def weave(engine_copy, woven, planes):
+    engine_copy(
+        woven[:].rearrange("p (c i t) -> p c t i", i=4, t=PACK),
+        planes[:].rearrange("p t (c i) -> p c t i", i=4),
+    )
+
+
+def tile_picked_keydifbig_none_po_kernel(
+    tc, x_words, x_scales, d_words, d_scales, gn, w1_words, w1_scales, offs, kidx, n1, n2, out_0, out_1, out_2
+):
+    nc = tc.nc
+    with ExitStack() as ctx:
+        lists = ctx.enter_context(tc.tile_pool(name="lists", bufs=1))
+        sb = ctx.enter_context(tc.tile_pool(name="sb", bufs=1))
+        psum = ctx.enter_context(tc.psum_pool(name="psum", bufs=1))
+
+        kidx_t = lists.tile([P, H // 16], U16, name="kidx_t")
+        offs_t = lists.tile([P, S // 16], U16, name="offs_t")
+        n1_t = lists.tile([P, S // 16], U16, name="n1_t")
+        n2_t = lists.tile([P, S // 16], U16, name="n2_t")
+        nc.sync.dma_start(kidx_t[:], kidx)
+
+        d_tab = sb.tile([P, G], U32, name="d_tab", align_bytes=64)
+        x_tab = sb.tile([P, T], U32, name="x_tab", align_bytes=64)
+
+        ds_tab = sb.tile([P, G], U8, name="ds_tab", align_bytes=64)
+        xs_tab = sb.tile([P, T], U8, name="xs_tab", align_bytes=64)
+        ws_raw = sb.tile([P, N], U8, name="ws_raw", align_bytes=64)
+        planes = sb.tile([P, H + S + N], U8, name="planes", align_bytes=64)
+        gn_t = sb.tile([P, PACK], F32, name="gn_t")
+        w_raw = sb.tile([P, N], U32, name="w_raw", align_bytes=64)
+        nc.vector.memset(xs_tab[:].bitcast(I32), 0)
+        nc.vector.memset(planes[:].bitcast(I32), 0)
+        nc.sync.dma_start(ds_tab[:].bitcast(I32), rows_of_blocks(d_scales))
+        nc.sync.dma_start(offs_t[:], offs)
+        nc.sync.dma_start(xs_tab[0:P:8, :].bitcast(I32), x_scales[0].bitcast(I32))
+        nc.sync.dma_start(ws_raw[:].bitcast(I32), rows_of_blocks(w1_scales))
+        nc.sync.dma_start(n1_t[:], n1)
+        nc.sync.dma_start(gn_t[:], gn.rearrange("(p t) o -> p (t o)", t=PACK))
+        nc.sync.dma_start(d_tab[:].bitcast(I32), words_view(d_words))
+        nc.sync.dma_start(x_tab[:].bitcast(I32), words_view(x_words))
+        nc.sync.dma_start(n2_t[:], n2)
+        nc.sync.dma_start(w_raw[:].bitcast(I32), words_view(w1_words))
+
+        gain = sb.tile([P, PACK], F32, name="gain")
+        nc.scalar.activation(gain[:], gn_t[:], COPY, scale=-0.0625)
+
+        ds_pick = sb.tile([P, H], U8, name="ds_pick", align_bytes=64)
+        xs_pick = sb.tile([P, S], U8, name="xs_pick", align_bytes=64)
+        spread = sb.tile([P, H + S + N], U8, name="spread", align_bytes=64)
+        nc.vector.tensor_copy(ds_pick[:], ds_tab[:].indirect(kidx_t[:]))
+        nc.vector.tensor_copy(xs_pick[:], xs_tab[:].indirect(offs_t[:]))
+        nc.vector.tensor_copy(
+            spread[:, :H].rearrange("p (t m) -> p t m", t=PACK), ds_pick[:].rearrange("p (m t) -> p t m", t=PACK)
+        )
+        nc.vector.tensor_copy(
+            spread[:, H + S :].rearrange("p (t m) -> p t m", t=PACK), ws_raw[:].rearrange("p (m t) -> p t m", t=PACK)
+        )
+        nc.vector.tensor_copy(spread[:, H : H + S].bitcast(I32), xs_pick[:].bitcast(I32))
+        for q in range(4):
+            nc.scalar.dma_start(
+                planes[32 * q : 32 * q + 4, :].bitcast(I32), spread[32 * q : 32 * q + 32 : 8, :].bitcast(I32)
+            )
+        ds_plane = planes[:, :H]
+        xs_plane = planes[:, H : H + S]
+        ws_plane = planes[:, H + S :]
+        d_pick = sb.tile([P, H], U32, name="d_pick", align_bytes=64)
+        d_dealt = sb.tile([P, H], U32, name="d_dealt", align_bytes=64)
+        nc.vector.tensor_copy(d_pick[:], d_tab[:].indirect(kidx_t[:]))
+        nc.vector.tensor_copy(
+            d_dealt[:].rearrange("p (t m) -> p t m", t=PACK), d_pick[:].rearrange("p (m t) -> p t m", t=PACK)
+        )
+
+        banks = [psum.tile([P, 512], F32, name=f"bank{b}") for b in range(8)]
+        s_win = [sb.tile([P, S], F32, name=f"s_win{t}") for t in range(PACK)]
+        s_own = [sb.tile([P, S], F32, name=f"s_own{t}") for t in range(PACK)]
+        for u in range(2):
+            x_pick = sb.tile([P, HALF], U32, name=f"x_pick{u}", align_bytes=64)
+            nc.vector.tensor_copy(x_pick[:], x_tab[:].indirect(offs_t[:, u * HALF // 16 : (u + 1) * HALF // 16]))
+            cols = slice(u * HALF, (u + 1) * HALF)
+            for t in range(PACK):
+                keys = slice(t * P, (t + 1) * P)
+                nc.tensor.matmul_mx(
+                    out=banks[4 * u + t][:, :HALF],
+                    lhsT=d_dealt[:, keys].bitcast(FP8X4),
+                    lhsT_scale=ds_plane[:, keys],
+                    rhs=x_pick[:].bitcast(FP8X4),
+                    rhs_scale=xs_plane[:, cols],
+                    start=True,
+                    stop=True,
+                )
+                nc.scalar.activation(s_win[t][:, cols], banks[4 * u + t][:, :HALF], COPY, scale=gain[:, t : t + 1])
+                if u == 1:
+                    nc.scalar.activation(s_own[t][:, :HALF], banks[t][:, :HALF], COPY, scale=gain[:, t : t + 1])
+        for t in range(PACK):
+            nc.scalar.activation(s_own[t][:, HALF:], banks[4 + t][:, :HALF], COPY, scale=gain[:, t : t + 1])
+
+        w_dealt = sb.tile([P, N], U32, name="w_dealt", align_bytes=64)
+        nc.vector.tensor_copy(
+            w_dealt[:].rearrange("p (t m) -> p t m", t=PACK), w_raw[:].rearrange("p (m t) -> p t m", t=PACK)
+        )
+
+        h_win = [sb.tile([P, S], F32, name=f"h_win{t}") for t in range(PACK)]
+
+        def finish_z(c, lo, hi, z):
+            width = hi - lo
+            last = c == len(PIECES1) - 1
+            z_woven = sb.tile([P, PACK * width], BF16, name=f"z_woven{c}", tag=f"zw{c}", align_bytes=64)
+            weave(nc.vector.tensor_copy if last else nc.scalar.copy, z_woven, z)
+            z_words = sb.tile([P, width], U32, name=f"z_words{c}", align_bytes=64)
+            z_plane = sb.tile([P, width], U8, name=f"z_plane{c}", align_bytes=64)
+            nc.vector.quantize_mx(out=z_words[:].bitcast(FP8X4), scales=z_plane[:], in_=z_woven[:])
+            for t in range(PACK):
+                rows = slice(t * P, (t + 1) * P)
+                bank = banks[4 * (c % 2) + t]
+                nc.tensor.matmul_mx(
+                    out=bank[:, :width],
+                    lhsT=w_dealt[:, rows].bitcast(FP8X4),
+                    lhsT_scale=ws_plane[:, rows],
+                    rhs=z_words[:].bitcast(FP8X4),
+                    rhs_scale=z_plane[:],
+                    start=True,
+                    stop=True,
+                )
+                nc.scalar.copy(h_win[t][:, lo:hi], bank[:, :width])
+
+        pending = None
+        for c, (lo, hi) in enumerate(PIECES1):
+            width = hi - lo
+            z = sb.tile([P, PACK, width], F32, name=f"z{c}", tag=f"zw{c - 2}", align_bytes=64)
+            for t in range(PACK):
+                far = s_win[t][:].indirect(n1_t[:, lo // 16 : hi // 16])
+                nc.vector.tensor_tensor(z[:, t, :], far, s_own[t][:, lo:hi], ALU.subtract)
+            if pending is not None:
+                finish_z(*pending)
+            pending = (c, lo, hi, z)
+        finish_z(*pending)
+
+        y_words = sb.tile([P, S], U32, name="y_words", align_bytes=64)
+        y_plane = sb.tile([P, S], U8, name="y_plane", align_bytes=64)
+        out_rows = out_0.rearrange("(p t) n -> p t n", t=PACK)
+
+        def finish_y(c, lo, hi, y):
+            width = hi - lo
+            last = c == len(PIECES2) - 1
+            y_woven = sb.tile([P, PACK * width], BF16, name=f"y_woven{c}", tag=f"yw{c}", align_bytes=64)
+            weave(nc.vector.tensor_copy if last else nc.scalar.copy, y_woven, y)
+            nc.vector.quantize_mx(out=y_words[:, lo:hi].bitcast(FP8X4), scales=y_plane[:, lo:hi], in_=y_woven[:])
+            nc.sync.dma_start(words_view(out_1)[:, lo:hi], y_words[:, lo:hi].bitcast(I32))
+
+        pending = None
+        for c, (lo, hi) in enumerate(PIECES2):
+            width = hi - lo
+            y = sb.tile([P, PACK, width], F32, name=f"y{c}")
+            h_far = sb.tile([P, PACK, width], F32, name=f"h_far{c}", tag=f"yw{c - 2}", align_bytes=64)
+            for t in range(PACK):
+                nc.vector.tensor_copy(h_far[:, t, :], h_win[t][:].indirect(n2_t[:, lo // 16 : hi // 16]))
+                if t > 0:
+                    nc.vector.tensor_tensor(y[:, t - 1, :], h_win[t - 1][:, lo:hi], h_far[:, t - 1, :], ALU.max)
+            nc.vector.tensor_tensor(y[:, PACK - 1, :], h_win[PACK - 1][:, lo:hi], h_far[:, PACK - 1, :], ALU.max)
+            nc.sync.dma_start(out_rows[:, :, lo:hi], y[:])
+            if pending is not None:
+                finish_y(*pending)
+            pending = (c, lo, hi, y)
+        finish_y(*pending)
+        for q in range(4):
+            queue = nc.scalar if q % 2 == 0 else nc.sync
+            queue.dma_start(out_2[0].bitcast(I32)[4 * q : 4 * q + 4, :], y_plane[32 * q : 32 * q + 4, :].bitcast(I32))

@@ -17,9 +17,11 @@ ALU = mybir.AluOpType
 
 P = 128
 PACK = 4
+LAST = PACK - 1
 HALF = S // 2
-PIECES1 = ((0, 256), (256, 384), (384, 512))
-PIECES2 = ((0, 256), (256, 384), (384, 512))
+HALVES = (slice(0, HALF), slice(HALF, S))
+LOW, HIGH, ALL = slice(0, 2), slice(2, 4), slice(0, 4)
+LIST_HALVES = (slice(0, HALF // 16), slice(HALF // 16, S // 16))
 
 
 def words_view(ap):
@@ -31,10 +33,22 @@ def rows_of_blocks(ap):
     return rows.unsqueeze(1).to_broadcast([16, 8, rows.shape[1]])
 
 
-def weave(engine_copy, woven, planes):
-    engine_copy(
-        woven[:].rearrange("p (c i t) -> p c t i", i=4, t=PACK),
-        planes[:].rearrange("p t (c i) -> p c t i", i=4),
+def deal(nc, dealt, plain, run):
+    nc.vector.tensor_copy(
+        dealt.rearrange("p (t c i) -> p c t i", t=PACK, i=run),
+        plain.rearrange("p (c i t) -> p c t i", t=PACK, i=run),
+    )
+
+
+def place_rows(queue, plane, spread):
+    for q in range(4):
+        queue.dma_start(plane[32 * q : 32 * q + 4, :].bitcast(I32), spread[32 * q : 32 * q + 32 : 8, :].bitcast(I32))
+
+
+def weave(copy, woven, planes, ts):
+    copy(
+        woven[:].rearrange("p (c i t) -> p c t i", i=4, t=PACK)[:, :, ts, :],
+        planes.rearrange("p t (c i) -> p c t i", i=4)[:, :, ts, :],
     )
 
 
@@ -51,151 +65,147 @@ def tile_picked_keydifbig_none_po_kernel(
         offs_t = lists.tile([P, S // 16], U16, name="offs_t")
         n1_t = lists.tile([P, S // 16], U16, name="n1_t")
         n2_t = lists.tile([P, S // 16], U16, name="n2_t")
-        nc.sync.dma_start(kidx_t[:], kidx)
-
         d_tab = sb.tile([P, G], U32, name="d_tab", align_bytes=64)
-        x_tab = sb.tile([P, T], U32, name="x_tab", align_bytes=64)
-
+        x_tab = sb.tile([P, T], U32, name="x_tab", tag="x_tab", align_bytes=64)
         ds_tab = sb.tile([P, G], U8, name="ds_tab", align_bytes=64)
         xs_tab = sb.tile([P, T], U8, name="xs_tab", align_bytes=64)
         ws_raw = sb.tile([P, N], U8, name="ws_raw", align_bytes=64)
-        planes = sb.tile([P, H + S + N], U8, name="planes", align_bytes=64)
         gn_t = sb.tile([P, PACK], F32, name="gn_t")
-        w_raw = sb.tile([P, N], U32, name="w_raw", align_bytes=64)
-        nc.vector.memset(xs_tab[:].bitcast(I32), 0)
-        nc.vector.memset(planes[:].bitcast(I32), 0)
+        nc.sync.dma_start(kidx_t[:], kidx)
         nc.sync.dma_start(ds_tab[:].bitcast(I32), rows_of_blocks(d_scales))
         nc.sync.dma_start(offs_t[:], offs)
-        nc.sync.dma_start(xs_tab[0:P:8, :].bitcast(I32), x_scales[0].bitcast(I32))
-        nc.sync.dma_start(ws_raw[:].bitcast(I32), rows_of_blocks(w1_scales))
-        nc.sync.dma_start(n1_t[:], n1)
+        nc.sync.dma_start(xs_tab[:].bitcast(I32), rows_of_blocks(x_scales))
         nc.sync.dma_start(gn_t[:], gn.rearrange("(p t) o -> p (t o)", t=PACK))
+        nc.sync.dma_start(n1_t[:], n1)
         nc.sync.dma_start(d_tab[:].bitcast(I32), words_view(d_words))
         nc.sync.dma_start(x_tab[:].bitcast(I32), words_view(x_words))
+        nc.sync.dma_start(ws_raw[:].bitcast(I32), rows_of_blocks(w1_scales))
         nc.sync.dma_start(n2_t[:], n2)
-        nc.sync.dma_start(w_raw[:].bitcast(I32), words_view(w1_words))
 
+        planes = sb.tile([P, H + S], U8, name="planes", align_bytes=64)
+        ws_plane = sb.tile([P, N], U8, name="ws_plane", align_bytes=64)
+        nc.vector.memset(planes[:].bitcast(I32), 0)
+        nc.vector.memset(ws_plane[:].bitcast(I32), 0)
+        win = [sb.tile([P, S if t == LAST else 2 * S], F32, name=f"win{t}") for t in range(PACK)]
+        for t in range(LAST):
+            nc.vector.memset(win[t][:, S:], 0.0)
+        warm = sb.tile([P, 2], F32, name="warm")
+        nc.gpsimd.memset(warm[:, 0:1], 0.0)
+        nc.scalar.activation(warm[:, 1:2], warm[:, 0:1], COPY)
         gain = sb.tile([P, PACK], F32, name="gain")
         nc.scalar.activation(gain[:], gn_t[:], COPY, scale=-0.0625)
 
         ds_pick = sb.tile([P, H], U8, name="ds_pick", align_bytes=64)
-        xs_pick = sb.tile([P, S], U8, name="xs_pick", align_bytes=64)
-        spread = sb.tile([P, H + S + N], U8, name="spread", align_bytes=64)
+        xs_pick = sb.tile([P, S], U8, name="xs_pick", tag="xs_pick", align_bytes=64)
+        spread = sb.tile([P, H + S], U8, name="spread", align_bytes=64)
         nc.vector.tensor_copy(ds_pick[:], ds_tab[:].indirect(kidx_t[:]))
         nc.vector.tensor_copy(xs_pick[:], xs_tab[:].indirect(offs_t[:]))
-        nc.vector.tensor_copy(
-            spread[:, :H].rearrange("p (t m) -> p t m", t=PACK), ds_pick[:].rearrange("p (m t) -> p t m", t=PACK)
-        )
-        nc.vector.tensor_copy(
-            spread[:, H + S :].rearrange("p (t m) -> p t m", t=PACK), ws_raw[:].rearrange("p (m t) -> p t m", t=PACK)
-        )
-        nc.vector.tensor_copy(spread[:, H : H + S].bitcast(I32), xs_pick[:].bitcast(I32))
-        for q in range(4):
-            nc.scalar.dma_start(
-                planes[32 * q : 32 * q + 4, :].bitcast(I32), spread[32 * q : 32 * q + 32 : 8, :].bitcast(I32)
-            )
+        deal(nc, spread[:, :H], ds_pick[:], 16)
+        nc.vector.tensor_copy(spread[:, H:].bitcast(I32), xs_pick[:].bitcast(I32))
+        place_rows(nc.scalar, planes, spread)
+        w_raw = sb.tile([P, N], U32, name="w_raw", tag="xs_pick", align_bytes=64)
+        nc.scalar.dma_start(w_raw[:].bitcast(I32), words_view(w1_words))
         ds_plane = planes[:, :H]
-        xs_plane = planes[:, H : H + S]
-        ws_plane = planes[:, H + S :]
+        xs_plane = planes[:, H:]
         d_pick = sb.tile([P, H], U32, name="d_pick", align_bytes=64)
         d_dealt = sb.tile([P, H], U32, name="d_dealt", align_bytes=64)
         nc.vector.tensor_copy(d_pick[:], d_tab[:].indirect(kidx_t[:]))
-        nc.vector.tensor_copy(
-            d_dealt[:].rearrange("p (t m) -> p t m", t=PACK), d_pick[:].rearrange("p (m t) -> p t m", t=PACK)
-        )
-
-        banks = [psum.tile([P, 512], F32, name=f"bank{b}") for b in range(8)]
-        s_win = [sb.tile([P, S], F32, name=f"s_win{t}") for t in range(PACK)]
-        s_own = [sb.tile([P, S], F32, name=f"s_own{t}") for t in range(PACK)]
+        deal(nc, d_dealt[:], d_pick[:], 4)
+        x_pick = [sb.tile([P, HALF], U32, name=f"x_pick{u}", align_bytes=64) for u in range(2)]
         for u in range(2):
-            x_pick = sb.tile([P, HALF], U32, name=f"x_pick{u}", align_bytes=64)
-            nc.vector.tensor_copy(x_pick[:], x_tab[:].indirect(offs_t[:, u * HALF // 16 : (u + 1) * HALF // 16]))
-            cols = slice(u * HALF, (u + 1) * HALF)
-            for t in range(PACK):
-                keys = slice(t * P, (t + 1) * P)
+            nc.vector.tensor_copy(x_pick[u][:], x_tab[:].indirect(offs_t[:, LIST_HALVES[u]]))
+
+        w_dealt = sb.tile([P, N], U32, name="w_dealt", tag="x_tab", align_bytes=64)
+        ws_dealt = sb.tile([P, N], U8, name="ws_dealt", align_bytes=64)
+        deal(nc, ws_dealt[:], ws_raw[:], 16)
+        place_rows(nc.sync, ws_plane, ws_dealt)
+        deal(nc, w_dealt[:], w_raw[:], 4)
+
+        banks = [psum.tile([P, S], F32, name=f"bank{b}") for b in range(8)]
+
+        own = [sb.tile([P, S], F32, name=f"own{t}") for t in range(PACK)]
+        for t in range(PACK):
+            keys = slice(t * P, (t + 1) * P)
+            scale = gain[:, t : t + 1]
+            for u in range(2):
+                bank = banks[4 + u] if t == 0 else banks[t]
                 nc.tensor.matmul_mx(
-                    out=banks[4 * u + t][:, :HALF],
+                    out=bank[:, HALVES[u]],
                     lhsT=d_dealt[:, keys].bitcast(FP8X4),
                     lhsT_scale=ds_plane[:, keys],
-                    rhs=x_pick[:].bitcast(FP8X4),
-                    rhs_scale=xs_plane[:, cols],
+                    rhs=x_pick[u][:].bitcast(FP8X4),
+                    rhs_scale=xs_plane[:, HALVES[u]],
                     start=True,
                     stop=True,
                 )
-                nc.scalar.activation(s_win[t][:, cols], banks[4 * u + t][:, :HALF], COPY, scale=gain[:, t : t + 1])
-                if u == 1:
-                    nc.scalar.activation(s_own[t][:, :HALF], banks[t][:, :HALF], COPY, scale=gain[:, t : t + 1])
+                if t == 0:
+                    nc.scalar.activation(win[t][:, HALVES[u]], bank[:, HALVES[u]], COPY, scale=scale)
+            if t == 0:
+                for u in range(2):
+                    nc.scalar.activation(own[t][:, HALVES[u]], banks[4 + u][:, HALVES[u]], COPY, scale=scale)
+            else:
+                nc.scalar.activation(win[t][:, :S], banks[t][:], COPY, scale=scale)
+                nc.scalar.activation(own[t][:], banks[t][:], COPY, scale=scale)
+
+        z = sb.tile([P, PACK, S], F32, name="z")
+        for t in range(LAST):
+            nc.vector.tensor_tensor(z[:, t, :], win[t][:].indirect(n1_t[:]), own[t][:], ALU.subtract)
+        z_woven = [sb.tile([P, PACK * HALF], BF16, name=f"z_woven{u}", align_bytes=64) for u in range(2)]
+        z_words = [sb.tile([P, HALF], U32, name=f"z_words{u}", align_bytes=64) for u in range(2)]
+        z_plane = [sb.tile([P, HALF], U8, name=f"z_plane{u}", align_bytes=64) for u in range(2)]
+        weave(nc.scalar.copy, z_woven[0], z[:, :, HALVES[0]], LOW)
+        for u in range(2):
+            far = win[LAST][:].indirect(n1_t[:, LIST_HALVES[u]])
+            nc.vector.tensor_tensor(z[:, LAST, HALVES[u]], far, own[LAST][:, HALVES[u]], ALU.subtract)
+            if u == 0:
+                weave(nc.scalar.copy, z_woven[u], z[:, :, HALVES[u]], HIGH)
+            else:
+                weave(nc.vector.tensor_copy, z_woven[u], z[:, :, HALVES[u]], ALL)
+        for u in range(2):
+            nc.vector.quantize_mx(out=z_words[u][:].bitcast(FP8X4), scales=z_plane[u][:], in_=z_woven[u][:])
+
         for t in range(PACK):
-            nc.scalar.activation(s_own[t][:, HALF:], banks[4 + t][:, :HALF], COPY, scale=gain[:, t : t + 1])
-
-        w_dealt = sb.tile([P, N], U32, name="w_dealt", align_bytes=64)
-        nc.vector.tensor_copy(
-            w_dealt[:].rearrange("p (t m) -> p t m", t=PACK), w_raw[:].rearrange("p (m t) -> p t m", t=PACK)
-        )
-
-        h_win = [sb.tile([P, S], F32, name=f"h_win{t}") for t in range(PACK)]
-
-        def finish_z(c, lo, hi, z):
-            width = hi - lo
-            last = c == len(PIECES1) - 1
-            z_woven = sb.tile([P, PACK * width], BF16, name=f"z_woven{c}", tag=f"zw{c}", align_bytes=64)
-            weave(nc.vector.tensor_copy if last else nc.scalar.copy, z_woven, z)
-            z_words = sb.tile([P, width], U32, name=f"z_words{c}", align_bytes=64)
-            z_plane = sb.tile([P, width], U8, name=f"z_plane{c}", align_bytes=64)
-            nc.vector.quantize_mx(out=z_words[:].bitcast(FP8X4), scales=z_plane[:], in_=z_woven[:])
-            for t in range(PACK):
-                rows = slice(t * P, (t + 1) * P)
-                bank = banks[4 * (c % 2) + t]
+            rows = slice(t * P, (t + 1) * P)
+            for u in range(2):
+                bank = banks[t + 3 + u]
                 nc.tensor.matmul_mx(
-                    out=bank[:, :width],
+                    out=bank[:, HALVES[u]],
                     lhsT=w_dealt[:, rows].bitcast(FP8X4),
                     lhsT_scale=ws_plane[:, rows],
-                    rhs=z_words[:].bitcast(FP8X4),
-                    rhs_scale=z_plane[:],
+                    rhs=z_words[u][:].bitcast(FP8X4),
+                    rhs_scale=z_plane[u][:],
                     start=True,
                     stop=True,
                 )
-                nc.scalar.copy(h_win[t][:, lo:hi], bank[:, :width])
+                nc.scalar.copy(win[t][:, HALVES[u]], bank[:, HALVES[u]])
 
-        pending = None
-        for c, (lo, hi) in enumerate(PIECES1):
-            width = hi - lo
-            z = sb.tile([P, PACK, width], F32, name=f"z{c}", tag=f"zw{c - 2}", align_bytes=64)
-            for t in range(PACK):
-                far = s_win[t][:].indirect(n1_t[:, lo // 16 : hi // 16])
-                nc.vector.tensor_tensor(z[:, t, :], far, s_own[t][:, lo:hi], ALU.subtract)
-            if pending is not None:
-                finish_z(*pending)
-            pending = (c, lo, hi, z)
-        finish_z(*pending)
-
+        y = sb.tile([P, PACK, S], F32, name="y")
+        h_far = sb.tile([P, PACK, S], F32, name="h_far")
+        out_rows = out_0.rearrange("(p t) n -> p t n", t=PACK)
+        for t in range(LAST):
+            nc.vector.tensor_copy(h_far[:, t, :], win[t][:].indirect(n2_t[:]))
+            if t > 0:
+                nc.vector.tensor_tensor(y[:, t - 1, :], win[t - 1][:, :S], h_far[:, t - 1, :], ALU.max)
+                nc.sync.dma_start(out_rows[:, t - 1, :], y[:, t - 1, :])
+        nc.vector.tensor_copy(h_far[:, LAST, HALVES[0]], win[LAST][:].indirect(n2_t[:, LIST_HALVES[0]]))
+        nc.vector.tensor_tensor(y[:, LAST - 1, :], win[LAST - 1][:, :S], h_far[:, LAST - 1, :], ALU.max)
+        nc.sync.dma_start(out_rows[:, LAST - 1, :], y[:, LAST - 1, :])
+        y_woven = [sb.tile([P, PACK * HALF], BF16, name=f"y_woven{u}", align_bytes=64) for u in range(2)]
         y_words = sb.tile([P, S], U32, name="y_words", align_bytes=64)
         y_plane = sb.tile([P, S], U8, name="y_plane", align_bytes=64)
-        out_rows = out_0.rearrange("(p t) n -> p t n", t=PACK)
-
-        def finish_y(c, lo, hi, y):
-            width = hi - lo
-            last = c == len(PIECES2) - 1
-            y_woven = sb.tile([P, PACK * width], BF16, name=f"y_woven{c}", tag=f"yw{c}", align_bytes=64)
-            weave(nc.vector.tensor_copy if last else nc.scalar.copy, y_woven, y)
-            nc.vector.quantize_mx(out=y_words[:, lo:hi].bitcast(FP8X4), scales=y_plane[:, lo:hi], in_=y_woven[:])
-            nc.sync.dma_start(words_view(out_1)[:, lo:hi], y_words[:, lo:hi].bitcast(I32))
-
-        pending = None
-        for c, (lo, hi) in enumerate(PIECES2):
-            width = hi - lo
-            y = sb.tile([P, PACK, width], F32, name=f"y{c}")
-            h_far = sb.tile([P, PACK, width], F32, name=f"h_far{c}", tag=f"yw{c - 2}", align_bytes=64)
-            for t in range(PACK):
-                nc.vector.tensor_copy(h_far[:, t, :], h_win[t][:].indirect(n2_t[:, lo // 16 : hi // 16]))
-                if t > 0:
-                    nc.vector.tensor_tensor(y[:, t - 1, :], h_win[t - 1][:, lo:hi], h_far[:, t - 1, :], ALU.max)
-            nc.vector.tensor_tensor(y[:, PACK - 1, :], h_win[PACK - 1][:, lo:hi], h_far[:, PACK - 1, :], ALU.max)
-            nc.sync.dma_start(out_rows[:, :, lo:hi], y[:])
-            if pending is not None:
-                finish_y(*pending)
-            pending = (c, lo, hi, y)
-        finish_y(*pending)
+        for u in range(2):
+            weave(nc.scalar.copy, y_woven[u], y[:, :, HALVES[u]], LOW)
+        for u in range(2):
+            cols = HALVES[u]
+            if u == 1:
+                nc.vector.tensor_copy(h_far[:, LAST, cols], win[LAST][:].indirect(n2_t[:, LIST_HALVES[u]]))
+            nc.vector.tensor_tensor(y[:, LAST, cols], win[LAST][:, cols], h_far[:, LAST, cols], ALU.max)
+            nc.sync.dma_start(out_rows[:, LAST, cols], y[:, LAST, cols])
+            weave(nc.scalar.copy if u == 0 else nc.vector.tensor_copy, y_woven[u], y[:, :, cols], HIGH)
+        for u in range(2):
+            cols = HALVES[u]
+            nc.vector.quantize_mx(out=y_words[:, cols].bitcast(FP8X4), scales=y_plane[:, cols], in_=y_woven[u][:])
+            nc.sync.dma_start(words_view(out_1)[:, cols], y_words[:, cols].bitcast(I32))
         for q in range(4):
-            queue = nc.scalar if q % 2 == 0 else nc.sync
+            queue = nc.scalar if q < 3 else nc.sync
             queue.dma_start(out_2[0].bitcast(I32)[4 * q : 4 * q + 4, :], y_plane[32 * q : 32 * q + 4, :].bitcast(I32))

@@ -28,9 +28,9 @@ def words_view(ap):
     return ap[0].rearrange("p n r -> p (n r)").bitcast(I32)
 
 
-def rows_of_blocks(ap):
-    rows = ap[0].bitcast(I32)
-    return rows.unsqueeze(1).to_broadcast([16, 8, rows.shape[1]])
+def load_rows(nc, tile, scales):
+    nc.vector.memset(tile[:].bitcast(I32), 0)
+    nc.scalar.dma_start(tile[0:P:8, :].bitcast(I32), scales[0].bitcast(I32))
 
 
 def deal(nc, dealt, plain, run):
@@ -72,15 +72,15 @@ def tile_picked_keydifbig_none_po_kernel(
         ws_raw = sb.tile([P, N], U8, name="ws_raw", align_bytes=64)
         gn_t = sb.tile([P, PACK], F32, name="gn_t")
         nc.sync.dma_start(kidx_t[:], kidx)
-        nc.sync.dma_start(ds_tab[:].bitcast(I32), rows_of_blocks(d_scales))
         nc.sync.dma_start(offs_t[:], offs)
-        nc.sync.dma_start(xs_tab[:].bitcast(I32), rows_of_blocks(x_scales))
-        nc.sync.dma_start(gn_t[:], gn.rearrange("(p t) o -> p (t o)", t=PACK))
         nc.sync.dma_start(n1_t[:], n1)
+        nc.sync.dma_start(n2_t[:], n2)
         nc.sync.dma_start(d_tab[:].bitcast(I32), words_view(d_words))
         nc.sync.dma_start(x_tab[:].bitcast(I32), words_view(x_words))
-        nc.sync.dma_start(ws_raw[:].bitcast(I32), rows_of_blocks(w1_scales))
-        nc.sync.dma_start(n2_t[:], n2)
+        nc.gpsimd.dma_start(gn_t[:], gn.rearrange("(p t) o -> p (t o)", t=PACK))
+        load_rows(nc, ds_tab, d_scales)
+        load_rows(nc, xs_tab, x_scales)
+        load_rows(nc, ws_raw, w1_scales)
 
         planes = sb.tile([P, H + S], U8, name="planes", align_bytes=64)
         ws_plane = sb.tile([P, N], U8, name="ws_plane", align_bytes=64)
@@ -90,7 +90,7 @@ def tile_picked_keydifbig_none_po_kernel(
         for t in range(LAST):
             nc.vector.memset(win[t][:, S:], 0.0)
         warm = sb.tile([P, 2], F32, name="warm")
-        nc.gpsimd.memset(warm[:, 0:1], 0.0)
+        nc.vector.memset(warm[:, 0:1], 0.0)
         nc.scalar.activation(warm[:, 1:2], warm[:, 0:1], COPY)
         gain = sb.tile([P, PACK], F32, name="gain")
         nc.scalar.activation(gain[:], gn_t[:], COPY, scale=-0.0625)
@@ -107,7 +107,7 @@ def tile_picked_keydifbig_none_po_kernel(
         nc.scalar.dma_start(w_raw[:].bitcast(I32), words_view(w1_words))
         ds_plane = planes[:, :H]
         xs_plane = planes[:, H:]
-        d_pick = sb.tile([P, H], U32, name="d_pick", align_bytes=64)
+        d_pick = sb.tile([P, H], U32, name="d_pick", tag="d_pick", align_bytes=64)
         d_dealt = sb.tile([P, H], U32, name="d_dealt", align_bytes=64)
         nc.vector.tensor_copy(d_pick[:], d_tab[:].indirect(kidx_t[:]))
         deal(nc, d_dealt[:], d_pick[:], 4)
@@ -116,7 +116,7 @@ def tile_picked_keydifbig_none_po_kernel(
             nc.vector.tensor_copy(x_pick[u][:], x_tab[:].indirect(offs_t[:, LIST_HALVES[u]]))
 
         w_dealt = sb.tile([P, N], U32, name="w_dealt", tag="x_tab", align_bytes=64)
-        ws_dealt = sb.tile([P, N], U8, name="ws_dealt", align_bytes=64)
+        ws_dealt = sb.tile([P, N], U8, name="ws_dealt", tag="d_pick", align_bytes=64)
         deal(nc, ws_dealt[:], ws_raw[:], 16)
         place_rows(nc.sync, ws_plane, ws_dealt)
         deal(nc, w_dealt[:], w_raw[:], 4)

@@ -59,6 +59,7 @@ def tile_picked_keydifbig_none_po_kernel(
     with ExitStack() as ctx:
         lists = ctx.enter_context(tc.tile_pool(name="lists", bufs=1))
         sb = ctx.enter_context(tc.tile_pool(name="sb", bufs=1))
+        reuse = ctx.enter_context(tc.tile_pool(name="reuse", bufs=1))
         psum = ctx.enter_context(tc.psum_pool(name="psum", bufs=1))
 
         kidx_t = lists.tile([P, H // 16], U16, name="kidx_t")
@@ -66,7 +67,7 @@ def tile_picked_keydifbig_none_po_kernel(
         n1_t = lists.tile([P, S // 16], U16, name="n1_t")
         n2_t = lists.tile([P, S // 16], U16, name="n2_t")
         d_tab = sb.tile([P, G], U32, name="d_tab", align_bytes=64)
-        x_tab = sb.tile([P, T], U32, name="x_tab", tag="x_tab", align_bytes=64)
+        x_tab = reuse.tile([P, T], U32, name="x_tab", align_bytes=64, offset=0)
         ds_tab = sb.tile([P, G], U8, name="ds_tab", align_bytes=64)
         xs_tab = sb.tile([P, T], U8, name="xs_tab", align_bytes=64)
         ws_raw = sb.tile([P, N], U8, name="ws_raw", align_bytes=64)
@@ -107,7 +108,7 @@ def tile_picked_keydifbig_none_po_kernel(
         nc.scalar.dma_start(w_raw[:].bitcast(I32), words_view(w1_words))
         ds_plane = planes[:, :H]
         xs_plane = planes[:, H:]
-        d_pick = sb.tile([P, H], U32, name="d_pick", tag="d_pick", align_bytes=64)
+        d_pick = sb.tile([P, H], U32, name="d_pick", align_bytes=64)
         d_dealt = sb.tile([P, H], U32, name="d_dealt", align_bytes=64)
         nc.vector.tensor_copy(d_pick[:], d_tab[:].indirect(kidx_t[:]))
         deal(nc, d_dealt[:], d_pick[:], 4)
@@ -115,13 +116,13 @@ def tile_picked_keydifbig_none_po_kernel(
         for u in range(2):
             nc.vector.tensor_copy(x_pick[u][:], x_tab[:].indirect(offs_t[:, LIST_HALVES[u]]))
 
-        w_dealt = sb.tile([P, N], U32, name="w_dealt", tag="x_tab", align_bytes=64)
-        ws_dealt = sb.tile([P, N], U8, name="ws_dealt", tag="d_pick", align_bytes=64)
+        w_dealt = reuse.tile([P, N], U32, name="w_dealt", align_bytes=64, offset=0)
+        ws_dealt = reuse.tile([P, N], U8, name="ws_dealt", align_bytes=64, offset=4 * N)
         deal(nc, ws_dealt[:], ws_raw[:], 16)
         place_rows(nc.sync, ws_plane, ws_dealt)
         deal(nc, w_dealt[:], w_raw[:], 4)
 
-        banks = [psum.tile([P, S], F32, name=f"bank{b}") for b in range(8)]
+        banks = [psum.tile([P, S], F32, name=f"bank{b}") for b in range(6)]
 
         own = [sb.tile([P, S], F32, name=f"own{t}") for t in range(PACK)]
         for t in range(PACK):
@@ -151,8 +152,8 @@ def tile_picked_keydifbig_none_po_kernel(
         for t in range(LAST):
             nc.vector.tensor_tensor(z[:, t, :], win[t][:].indirect(n1_t[:]), own[t][:], ALU.subtract)
         z_woven = [sb.tile([P, PACK * HALF], BF16, name=f"z_woven{u}", align_bytes=64) for u in range(2)]
-        z_words = [sb.tile([P, HALF], U32, name=f"z_words{u}", align_bytes=64) for u in range(2)]
-        z_plane = [sb.tile([P, HALF], U8, name=f"z_plane{u}", align_bytes=64) for u in range(2)]
+        z_words = sb.tile([P, S], U32, name="z_words", align_bytes=64)
+        z_plane = sb.tile([P, S], U8, name="z_plane", align_bytes=64)
         weave(nc.scalar.copy, z_woven[0], z[:, :, HALVES[0]], LOW)
         for u in range(2):
             far = win[LAST][:].indirect(n1_t[:, LIST_HALVES[u]])
@@ -162,22 +163,23 @@ def tile_picked_keydifbig_none_po_kernel(
             else:
                 weave(nc.vector.tensor_copy, z_woven[u], z[:, :, HALVES[u]], ALL)
         for u in range(2):
-            nc.vector.quantize_mx(out=z_words[u][:].bitcast(FP8X4), scales=z_plane[u][:], in_=z_woven[u][:])
+            cols = HALVES[u]
+            nc.vector.quantize_mx(out=z_words[:, cols].bitcast(FP8X4), scales=z_plane[:, cols], in_=z_woven[u][:])
 
         for t in range(PACK):
             rows = slice(t * P, (t + 1) * P)
-            for u in range(2):
-                bank = banks[t + 3 + u]
+            parts = [(banks[4 + u], HALVES[u]) for u in range(2)] if t == 0 else [(banks[t], slice(0, S))]
+            for bank, cols in parts:
                 nc.tensor.matmul_mx(
-                    out=bank[:, HALVES[u]],
+                    out=bank[:, cols],
                     lhsT=w_dealt[:, rows].bitcast(FP8X4),
                     lhsT_scale=ws_plane[:, rows],
-                    rhs=z_words[u][:].bitcast(FP8X4),
-                    rhs_scale=z_plane[u][:],
+                    rhs=z_words[:, cols].bitcast(FP8X4),
+                    rhs_scale=z_plane[:, cols],
                     start=True,
                     stop=True,
                 )
-                nc.scalar.copy(win[t][:, HALVES[u]], bank[:, HALVES[u]])
+                nc.scalar.copy(win[t][:, cols], bank[:, cols])
 
         y = sb.tile([P, PACK, S], F32, name="y")
         h_far = sb.tile([P, PACK, S], F32, name="h_far")
@@ -190,6 +192,7 @@ def tile_picked_keydifbig_none_po_kernel(
         nc.vector.tensor_copy(h_far[:, LAST, HALVES[0]], win[LAST][:].indirect(n2_t[:, LIST_HALVES[0]]))
         nc.vector.tensor_tensor(y[:, LAST - 1, :], win[LAST - 1][:, :S], h_far[:, LAST - 1, :], ALU.max)
         nc.sync.dma_start(out_rows[:, LAST - 1, :], y[:, LAST - 1, :])
+        nc.vector.tensor_copy(h_far[:, LAST, HALVES[1]], win[LAST][:].indirect(n2_t[:, LIST_HALVES[1]]))
         y_woven = [sb.tile([P, PACK * HALF], BF16, name=f"y_woven{u}", align_bytes=64) for u in range(2)]
         y_words = sb.tile([P, S], U32, name="y_words", align_bytes=64)
         y_plane = sb.tile([P, S], U8, name="y_plane", align_bytes=64)
@@ -197,8 +200,6 @@ def tile_picked_keydifbig_none_po_kernel(
             weave(nc.scalar.copy, y_woven[u], y[:, :, HALVES[u]], LOW)
         for u in range(2):
             cols = HALVES[u]
-            if u == 1:
-                nc.vector.tensor_copy(h_far[:, LAST, cols], win[LAST][:].indirect(n2_t[:, LIST_HALVES[u]]))
             nc.vector.tensor_tensor(y[:, LAST, cols], win[LAST][:, cols], h_far[:, LAST, cols], ALU.max)
             nc.sync.dma_start(out_rows[:, LAST, cols], y[:, LAST, cols])
             weave(nc.scalar.copy if u == 0 else nc.vector.tensor_copy, y_woven[u], y[:, :, cols], HIGH)

@@ -30,7 +30,7 @@ def words_view(ap):
 
 def load_rows(nc, tile, scales):
     nc.vector.memset(tile[:].bitcast(I32), 0)
-    nc.scalar.dma_start(tile[0:P:8, :].bitcast(I32), scales[0].bitcast(I32))
+    nc.sync.dma_start(tile[0:P:8, :].bitcast(I32), scales[0].bitcast(I32))
 
 
 def deal(nc, dealt, plain, run):
@@ -66,8 +66,6 @@ def tile_picked_keydifbig_none_po_kernel(
         offs_t = lists.tile([P, S // 16], U16, name="offs_t")
         n1_t = lists.tile([P, S // 16], U16, name="n1_t")
         n2_t = lists.tile([P, S // 16], U16, name="n2_t")
-        d_tab = sb.tile([P, G], U32, name="d_tab", align_bytes=64)
-        x_tab = reuse.tile([P, T], U32, name="x_tab", align_bytes=64, offset=0)
         ds_tab = sb.tile([P, G], U8, name="ds_tab", align_bytes=64)
         xs_tab = sb.tile([P, T], U8, name="xs_tab", align_bytes=64)
         ws_raw = sb.tile([P, N], U8, name="ws_raw", align_bytes=64)
@@ -76,23 +74,27 @@ def tile_picked_keydifbig_none_po_kernel(
         nc.sync.dma_start(offs_t[:], offs)
         nc.sync.dma_start(n1_t[:], n1)
         nc.sync.dma_start(n2_t[:], n2)
+        nc.sync.dma_start(gn_t[:], gn.rearrange("(p t) o -> p (t o)", t=PACK))
+        load_rows(nc, ds_tab, d_scales)
+        zeros = reuse.tile([P, 32], F32, name="zeros", align_bytes=64, offset=4 * T - 64)
+        nc.vector.memset(zeros[:], 0.0)
+        load_rows(nc, xs_tab, x_scales)
+
+        win = [sb.tile([P, S if t == LAST else 2 * S], F32, name=f"win{t}") for t in range(PACK)]
+        nc.vector.tensor_copy(win[0][:, S : S + 32], zeros[:])
+        nc.vector.memset(win[0][:, S + 32 :], 0.0)
+        x_tab = reuse.tile([P, T], U32, name="x_tab", align_bytes=64, offset=0)
+        d_tab = reuse.tile([P, G], U32, name="d_tab", align_bytes=64, offset=4 * T)
         nc.sync.dma_start(d_tab[:].bitcast(I32), words_view(d_words))
         nc.sync.dma_start(x_tab[:].bitcast(I32), words_view(x_words))
-        nc.gpsimd.dma_start(gn_t[:], gn.rearrange("(p t) o -> p (t o)", t=PACK))
-        load_rows(nc, ds_tab, d_scales)
-        load_rows(nc, xs_tab, x_scales)
         load_rows(nc, ws_raw, w1_scales)
+        for t in range(1, LAST):
+            nc.scalar.activation(win[t][:, S:], win[0][:, S:], COPY)
 
         planes = sb.tile([P, H + S], U8, name="planes", align_bytes=64)
         ws_plane = sb.tile([P, N], U8, name="ws_plane", align_bytes=64)
         nc.vector.memset(planes[:].bitcast(I32), 0)
         nc.vector.memset(ws_plane[:].bitcast(I32), 0)
-        win = [sb.tile([P, S if t == LAST else 2 * S], F32, name=f"win{t}") for t in range(PACK)]
-        for t in range(LAST):
-            nc.vector.memset(win[t][:, S:], 0.0)
-        warm = sb.tile([P, 2], F32, name="warm")
-        nc.vector.memset(warm[:, 0:1], 0.0)
-        nc.scalar.activation(warm[:, 1:2], warm[:, 0:1], COPY)
         gain = sb.tile([P, PACK], F32, name="gain")
         nc.scalar.activation(gain[:], gn_t[:], COPY, scale=-0.0625)
 

from contextlib import ExitStack

import concourse.mybir as mybir

K, T, S, N, G, H = 512, 2048, 512, 512, 2048, 512
FLOPS = 2 * K * H * S + 2 * H * N * S

F32 = mybir.dt.float32
BF16 = mybir.dt.bfloat16
I32 = mybir.dt.int32
U32 = mybir.dt.uint32
U16 = mybir.dt.uint16
U8 = mybir.dt.uint8
FP8X4 = mybir.dt.float8_e4m3fn_x4
COPY = mybir.ActivationFunctionType.Copy
ALU = mybir.AluOpType

P = 128
PACK = 4
LAST = PACK - 1
HALF = S // 2
HALVES = (slice(0, HALF), slice(HALF, S))
LOW, HIGH, ALL = slice(0, 2), slice(2, 4), slice(0, 4)
LIST_HALVES = (slice(0, HALF // 16), slice(HALF // 16, S // 16))


def words_view(ap):
    return ap[0].rearrange("p n r -> p (n r)").bitcast(I32)


def load_rows(nc, tile, scales):
    nc.vector.memset(tile[:].bitcast(I32), 0)
    nc.sync.dma_start(tile[0:P:8, :].bitcast(I32), scales[0].bitcast(I32))


def deal(nc, dealt, plain, run):
    nc.vector.tensor_copy(
        dealt.rearrange("p (t c i) -> p c t i", t=PACK, i=run),
        plain.rearrange("p (c i t) -> p c t i", t=PACK, i=run),
    )


def place_rows(queue, plane, spread):
    for q in range(4):
        queue.dma_start(plane[32 * q : 32 * q + 4, :].bitcast(I32), spread[32 * q : 32 * q + 32 : 8, :].bitcast(I32))


def weave(copy, woven, planes, ts):
    copy(
        woven[:].rearrange("p (c i t) -> p c t i", i=4, t=PACK)[:, :, ts, :],
        planes.rearrange("p t (c i) -> p c t i", i=4)[:, :, ts, :],
    )


def tile_picked_keydifbig_none_po_kernel(
    tc, x_words, x_scales, d_words, d_scales, gn, w1_words, w1_scales, offs, kidx, n1, n2, out_0, out_1, out_2
):
    nc = tc.nc
    with ExitStack() as ctx:
        lists = ctx.enter_context(tc.tile_pool(name="lists", bufs=1))
        sb = ctx.enter_context(tc.tile_pool(name="sb", bufs=1))
        reuse = ctx.enter_context(tc.tile_pool(name="reuse", bufs=1))
        psum = ctx.enter_context(tc.psum_pool(name="psum", bufs=1))

        kidx_t = lists.tile([P, H // 16], U16, name="kidx_t")
        offs_t = lists.tile([P, S // 16], U16, name="offs_t")
        n1_t = lists.tile([P, S // 16], U16, name="n1_t")
        n2_t = lists.tile([P, S // 16], U16, name="n2_t")
        ds_tab = sb.tile([P, G], U8, name="ds_tab", align_bytes=64)
        xs_tab = sb.tile([P, T], U8, name="xs_tab", align_bytes=64)
        ws_raw = sb.tile([P, N], U8, name="ws_raw", align_bytes=64)
        gn_t = sb.tile([P, PACK], F32, name="gn_t")
        nc.sync.dma_start(kidx_t[:], kidx)
        nc.sync.dma_start(offs_t[:], offs)
        nc.sync.dma_start(n1_t[:], n1)
        nc.sync.dma_start(n2_t[:], n2)
        nc.sync.dma_start(gn_t[:], gn.rearrange("(p t) o -> p (t o)", t=PACK))
        load_rows(nc, ds_tab, d_scales)
        zeros = reuse.tile([P, 32], F32, name="zeros", align_bytes=64, offset=4 * T - 64)
        nc.vector.memset(zeros[:], 0.0)
        load_rows(nc, xs_tab, x_scales)

        win = [sb.tile([P, S if t == LAST else 2 * S], F32, name=f"win{t}") for t in range(PACK)]
        nc.vector.tensor_copy(win[0][:, S : S + 32], zeros[:])
        nc.vector.memset(win[0][:, S + 32 :], 0.0)
        x_tab = reuse.tile([P, T], U32, name="x_tab", align_bytes=64, offset=0)
        d_tab = reuse.tile([P, G], U32, name="d_tab", align_bytes=64, offset=4 * T)
        nc.sync.dma_start(d_tab[:].bitcast(I32), words_view(d_words))
        nc.sync.dma_start(x_tab[:].bitcast(I32), words_view(x_words))
        load_rows(nc, ws_raw, w1_scales)
        for t in range(1, LAST):
            nc.scalar.activation(win[t][:, S:], win[0][:, S:], COPY)

        planes = sb.tile([P, H + S], U8, name="planes", align_bytes=64)
        ws_plane = sb.tile([P, N], U8, name="ws_plane", align_bytes=64)
        nc.vector.memset(planes[:].bitcast(I32), 0)
        nc.vector.memset(ws_plane[:].bitcast(I32), 0)
        gain = sb.tile([P, PACK], F32, name="gain")
        nc.scalar.activation(gain[:], gn_t[:], COPY, scale=-0.0625)

        ds_pick = sb.tile([P, H], U8, name="ds_pick", align_bytes=64)
        xs_pick = sb.tile([P, S], U8, name="xs_pick", tag="xs_pick", align_bytes=64)
        spread = sb.tile([P, H + S], U8, name="spread", align_bytes=64)
        nc.vector.tensor_copy(ds_pick[:], ds_tab[:].indirect(kidx_t[:]))
        nc.vector.tensor_copy(xs_pick[:], xs_tab[:].indirect(offs_t[:]))
        deal(nc, spread[:, :H], ds_pick[:], 16)
        nc.vector.tensor_copy(spread[:, H:].bitcast(I32), xs_pick[:].bitcast(I32))
        place_rows(nc.scalar, planes, spread)
        w_raw = sb.tile([P, N], U32, name="w_raw", tag="xs_pick", align_bytes=64)
        nc.scalar.dma_start(w_raw[:].bitcast(I32), words_view(w1_words))
        ds_plane = planes[:, :H]
        xs_plane = planes[:, H:]
        d_pick = sb.tile([P, H], U32, name="d_pick", align_bytes=64)
        d_dealt = sb.tile([P, H], U32, name="d_dealt", align_bytes=64)
        nc.vector.tensor_copy(d_pick[:], d_tab[:].indirect(kidx_t[:]))
        deal(nc, d_dealt[:], d_pick[:], 4)
        x_pick = [sb.tile([P, HALF], U32, name=f"x_pick{u}", align_bytes=64) for u in range(2)]
        for u in range(2):
            nc.vector.tensor_copy(x_pick[u][:], x_tab[:].indirect(offs_t[:, LIST_HALVES[u]]))

        w_dealt = reuse.tile([P, N], U32, name="w_dealt", align_bytes=64, offset=0)
        ws_dealt = reuse.tile([P, N], U8, name="ws_dealt", align_bytes=64, offset=4 * N)
        deal(nc, ws_dealt[:], ws_raw[:], 16)
        place_rows(nc.sync, ws_plane, ws_dealt)
        deal(nc, w_dealt[:], w_raw[:], 4)

        banks = [psum.tile([P, S], F32, name=f"bank{b}") for b in range(6)]

        own = [sb.tile([P, S], F32, name=f"own{t}") for t in range(PACK)]
        for t in range(PACK):
            keys = slice(t * P, (t + 1) * P)
            scale = gain[:, t : t + 1]
            for u in range(2):
                bank = banks[4 + u] if t == 0 else banks[t]
                nc.tensor.matmul_mx(
                    out=bank[:, HALVES[u]],
                    lhsT=d_dealt[:, keys].bitcast(FP8X4),
                    lhsT_scale=ds_plane[:, keys],
                    rhs=x_pick[u][:].bitcast(FP8X4),
                    rhs_scale=xs_plane[:, HALVES[u]],
                    start=True,
                    stop=True,
                )
                if t == 0:
                    nc.scalar.activation(win[t][:, HALVES[u]], bank[:, HALVES[u]], COPY, scale=scale)
            if t == 0:
                for u in range(2):
                    nc.scalar.activation(own[t][:, HALVES[u]], banks[4 + u][:, HALVES[u]], COPY, scale=scale)
            else:
                nc.scalar.activation(win[t][:, :S], banks[t][:], COPY, scale=scale)
                nc.scalar.activation(own[t][:], banks[t][:], COPY, scale=scale)

        z = sb.tile([P, PACK, S], F32, name="z")
        for t in range(LAST):
            nc.vector.tensor_tensor(z[:, t, :], win[t][:].indirect(n1_t[:]), own[t][:], ALU.subtract)
        z_woven = [sb.tile([P, PACK * HALF], BF16, name=f"z_woven{u}", align_bytes=64) for u in range(2)]
        z_words = sb.tile([P, S], U32, name="z_words", align_bytes=64)
        z_plane = sb.tile([P, S], U8, name="z_plane", align_bytes=64)
        weave(nc.scalar.copy, z_woven[0], z[:, :, HALVES[0]], LOW)
        for u in range(2):
            far = win[LAST][:].indirect(n1_t[:, LIST_HALVES[u]])
            nc.vector.tensor_tensor(z[:, LAST, HALVES[u]], far, own[LAST][:, HALVES[u]], ALU.subtract)
            if u == 0:
                weave(nc.scalar.copy, z_woven[u], z[:, :, HALVES[u]], HIGH)
            else:
                weave(nc.vector.tensor_copy, z_woven[u], z[:, :, HALVES[u]], ALL)
        for u in range(2):
            cols = HALVES[u]
            nc.vector.quantize_mx(out=z_words[:, cols].bitcast(FP8X4), scales=z_plane[:, cols], in_=z_woven[u][:])

        for t in range(PACK):
            rows = slice(t * P, (t + 1) * P)
            parts = [(banks[4 + u], HALVES[u]) for u in range(2)] if t == 0 else [(banks[t], slice(0, S))]
            for bank, cols in parts:
                nc.tensor.matmul_mx(
                    out=bank[:, cols],
                    lhsT=w_dealt[:, rows].bitcast(FP8X4),
                    lhsT_scale=ws_plane[:, rows],
                    rhs=z_words[:, cols].bitcast(FP8X4),
                    rhs_scale=z_plane[:, cols],
                    start=True,
                    stop=True,
                )
                nc.scalar.copy(win[t][:, cols], bank[:, cols])

        y = sb.tile([P, PACK, S], F32, name="y")
        h_far = sb.tile([P, PACK, S], F32, name="h_far")
        out_rows = out_0.rearrange("(p t) n -> p t n", t=PACK)
        for t in range(LAST):
            nc.vector.tensor_copy(h_far[:, t, :], win[t][:].indirect(n2_t[:]))
            if t > 0:
                nc.vector.tensor_tensor(y[:, t - 1, :], win[t - 1][:, :S], h_far[:, t - 1, :], ALU.max)
                nc.sync.dma_start(out_rows[:, t - 1, :], y[:, t - 1, :])
        nc.vector.tensor_copy(h_far[:, LAST, HALVES[0]], win[LAST][:].indirect(n2_t[:, LIST_HALVES[0]]))
        nc.vector.tensor_tensor(y[:, LAST - 1, :], win[LAST - 1][:, :S], h_far[:, LAST - 1, :], ALU.max)
        nc.sync.dma_start(out_rows[:, LAST - 1, :], y[:, LAST - 1, :])
        nc.vector.tensor_copy(h_far[:, LAST, HALVES[1]], win[LAST][:].indirect(n2_t[:, LIST_HALVES[1]]))
        y_woven = [sb.tile([P, PACK * HALF], BF16, name=f"y_woven{u}", align_bytes=64) for u in range(2)]
        y_words = sb.tile([P, S], U32, name="y_words", align_bytes=64)
        y_plane = sb.tile([P, S], U8, name="y_plane", align_bytes=64)
        for u in range(2):
            weave(nc.scalar.copy, y_woven[u], y[:, :, HALVES[u]], LOW)
        for u in range(2):
            cols = HALVES[u]
            nc.vector.tensor_tensor(y[:, LAST, cols], win[LAST][:, cols], h_far[:, LAST, cols], ALU.max)
            nc.sync.dma_start(out_rows[:, LAST, cols], y[:, LAST, cols])
            weave(nc.scalar.copy if u == 0 else nc.vector.tensor_copy, y_woven[u], y[:, :, cols], HIGH)
        for u in range(2):
            cols = HALVES[u]
            nc.vector.quantize_mx(out=y_words[:, cols].bitcast(FP8X4), scales=y_plane[:, cols], in_=y_woven[u][:])
            nc.sync.dma_start(words_view(out_1)[:, cols], y_words[:, cols].bitcast(I32))
        for q in range(4):
            queue = nc.scalar if q < 3 else nc.sync
            queue.dma_start(out_2[0].bitcast(I32)[4 * q : 4 * q + 4, :], y_plane[32 * q : 32 * q + 4, :].bitcast(I32))
